import numpy as np
import ml_dtypes

BF16 = ml_dtypes.bfloat16


def bf(x):
    return np.asarray(x, np.float32).astype(BF16)


def f32(x):
    return np.asarray(x, np.float32)


def f64(x):
    return np.asarray(x).astype(np.float64)


def striped(idx):
    return np.tile(idx.reshape(-1, 16).T, (8, 1))


S, K, M, N, E, Q, V, D = 256, 256, 256, 192, 2, 96, 128, 2


def setup_inputs():
    return {"base": bf(np.random.standard_normal((M, S))), "x": bf(np.random.standard_normal((K, N))), "w": bf(1.5 * np.random.standard_normal((E, K, M)) / np.sqrt(K)), "offs": striped(np.random.permutation(S)[:N])}


def reference(base, x, w, offs):
    idx = offs[:16].T.reshape(-1)
    z = f64(base).copy()
    for e in range(E):
        z[:, idx[e * Q : (e + 1) * Q]] += f64(w)[e].T @ f64(x)[:, e * Q : (e + 1) * Q]
    z = z
    return z.reshape(M, V, D).max(axis=2)

@@ -1,0 +1,58 @@
+import concourse.mybir as mybir
+from concourse.masks import make_identity
+
+P = 128
+M, S = 256, 256
+K, N = 256, 192
+E = 2
+Q = N // E
+D = 2
+MB, KB = M // P, K // P
+LIST_COLUMN = 16
+
+FLOPS = 2 * K * M * N
+
+BF16, F32, U16 = mybir.dt.bfloat16, mybir.dt.float32, mybir.dt.uint16
+
+
+def tile_rows_unpool_max_none_kernel(tc, base, x, w, offs, out):
+    nc = tc.nc
+    with tc.tile_pool(name="held", bufs=1) as held, tc.psum_pool(name="psum", bufs=1) as psum:
+        base_rows = held.tile([P, MB, S], BF16, name="base_rows")
+        offsets = held.tile([P, N // LIST_COLUMN], U16, name="offsets")
+        points = held.tile([P, KB, N], BF16, name="points")
+        weights = held.tile([P, E, KB, M], BF16, name="weights")
+        identity = held.tile([P, P], BF16, name="identity")
+        pooled = held.tile([P, MB, S // D], F32, name="pooled")
+        windows = [psum.tile([P, S], F32, name=f"window{b}") for b in range(MB)]
+
+        nc.sync.dma_start(base_rows[:], base.rearrange("(b p) s -> p b s", p=P))
+        nc.sync.dma_start(offsets[:], offs)
+        nc.sync.dma_start(points[:], x.rearrange("(p i) n -> p i n", i=KB))
+        for e in range(E):
+            nc.sync.dma_start(weights[:, e, :, :], w[e, :, :].rearrange("(p i) m -> p i m", i=KB))
+        make_identity(nc, identity[:])
+
+        for b in range(MB):
+            nc.tensor.matmul(windows[b][:], identity[:], base_rows[:, b, :], start=True, stop=False)
+
+        for e in range(E):
+            piece = offsets[:, e * Q // LIST_COLUMN : (e + 1) * Q // LIST_COLUMN]
+            for b in range(MB):
+                for i in range(KB):
+                    nc.tensor.matmul(
+                        windows[b][:].indirect(piece),
+                        weights[:, e, i, b * P : (b + 1) * P],
+                        points[:, i, e * Q : (e + 1) * Q],
+                        start=False,
+                        stop=(e == E - 1 and i == KB - 1),
+                    )
+
+        for b in range(MB):
+            nc.vector.tensor_reduce(
+                out=pooled[:, b, :],
+                in_=windows[b][:].rearrange("p (v d) -> p v d", d=D),
+                axis=mybir.AxisListType.X,
+                op=mybir.AluOpType.max,
+            )
+            nc.sync.dma_start(out[b * P : (b + 1) * P, :], pooled[:, b, :])

@@ -7,6 +7,8 @@ K, N = 256, 192
 E = 2
 Q = N // E
 D = 2
+BANK = 512
+WARM = 4
 MB, KB = M // P, K // P
 LIST_COLUMN = 16
 
@@ -24,6 +26,8 @@ def tile_rows_unpool_max_none_kernel(tc, base, x, w, offs, out):
         weights = held.tile([P, E, KB, M], BF16, name="weights")
         identity = held.tile([P, P], BF16, name="identity")
         pooled = held.tile([P, MB, S // D], F32, name="pooled")
+        blank = held.tile([P, BANK], BF16, name="blank")
+        warm_bank = psum.tile([P, BANK], F32, name="warm_bank")
         windows = [psum.tile([P, S], F32, name=f"window{b}") for b in range(MB)]
 
         nc.sync.dma_start(base_rows[:], base.rearrange("(b p) s -> p b s", p=P))
@@ -32,6 +36,10 @@ def tile_rows_unpool_max_none_kernel(tc, base, x, w, offs, out):
         for e in range(E):
             nc.sync.dma_start(weights[:, e, :, :], w[e, :, :].rearrange("(p i) m -> p i m", i=KB))
         make_identity(nc, identity[:])
+
+        nc.vector.memset(blank[:], 0.0)
+        for i in range(WARM):
+            nc.tensor.matmul(warm_bank[:], blank[:, :P], blank[:], start=True, stop=True)
 
         for b in range(MB):
             nc.tensor.matmul(windows[b][:], identity[:], base_rows[:, b, :], start=True, stop=False)

import concourse.mybir as mybir
from concourse.masks import make_identity

P = 128
M, S = 256, 256
K, N = 256, 192
E = 2
Q = N // E
D = 2
BANK = 512
WARM = 4
MB, KB = M // P, K // P
LIST_COLUMN = 16

FLOPS = 2 * K * M * N

BF16, F32, U16 = mybir.dt.bfloat16, mybir.dt.float32, mybir.dt.uint16


def tile_rows_unpool_max_none_kernel(tc, base, x, w, offs, out):
    nc = tc.nc
    with tc.tile_pool(name="held", bufs=1) as held, tc.psum_pool(name="psum", bufs=1) as psum:
        base_rows = held.tile([P, MB, S], BF16, name="base_rows")
        offsets = held.tile([P, N // LIST_COLUMN], U16, name="offsets")
        points = held.tile([P, KB, N], BF16, name="points")
        weights = held.tile([P, E, KB, M], BF16, name="weights")
        identity = held.tile([P, P], BF16, name="identity")
        pooled = held.tile([P, MB, S // D], F32, name="pooled")
        blank = held.tile([P, BANK], BF16, name="blank")
        warm_bank = psum.tile([P, BANK], F32, name="warm_bank")
        windows = [psum.tile([P, S], F32, name=f"window{b}") for b in range(MB)]

        nc.sync.dma_start(base_rows[:], base.rearrange("(b p) s -> p b s", p=P))
        nc.sync.dma_start(offsets[:], offs)
        nc.sync.dma_start(points[:], x.rearrange("(p i) n -> p i n", i=KB))
        for e in range(E):
            nc.sync.dma_start(weights[:, e, :, :], w[e, :, :].rearrange("(p i) m -> p i m", i=KB))
        make_identity(nc, identity[:])

        nc.vector.memset(blank[:], 0.0)
        for i in range(WARM):
            nc.tensor.matmul(warm_bank[:], blank[:, :P], blank[:], start=True, stop=True)

        for b in range(MB):
            nc.tensor.matmul(windows[b][:], identity[:], base_rows[:, b, :], start=True, stop=False)

        for e in range(E):
            piece = offsets[:, e * Q // LIST_COLUMN : (e + 1) * Q // LIST_COLUMN]
            for b in range(MB):
                for i in range(KB):
                    nc.tensor.matmul(
                        windows[b][:].indirect(piece),
                        weights[:, e, i, b * P : (b + 1) * P],
                        points[:, i, e * Q : (e + 1) * Q],
                        start=False,
                        stop=(e == E - 1 and i == KB - 1),
                    )

        for b in range(MB):
            nc.vector.tensor_reduce(
                out=pooled[:, b, :],
                in_=windows[b][:].rearrange("p (v d) -> p v d", d=D),
                axis=mybir.AxisListType.X,
                op=mybir.AluOpType.max,
            )
            nc.sync.dma_start(out[b * P : (b + 1) * P, :], pooled[:, b, :])
